import numpy as np, ml_dtypes
CORES = [36,164,52,180,100,228,116,244]
N = 8
import mx_ref
BF = ml_dtypes.bfloat16
def cols(t, e):
    v = np.concatenate([t.reshape(128, -1, 4), np.zeros((128, 1, 4), BF)], axis=1)
    return np.ascontiguousarray(v[:, e]).reshape(128, -1)
def cut(t, i, w=512):
    return t[:, w * i:w * i + w]
def pick(q, e):
    c = np.concatenate([q[0].reshape(128, -1, 4), np.zeros((128, 1, 4), np.uint8)], axis=1); s = np.concatenate([q[1], np.ones((16, 1), np.uint8)], axis=1)
    return (np.ascontiguousarray(c[:, e].reshape(128, -1)), np.ascontiguousarray(s[:, e]))
def join(*qs):
    return (np.concatenate([q[0] for q in qs], axis=1), np.concatenate([q[1] for q in qs], axis=1))
def put(q, e, v):
    c, s = q[0].reshape(128, -1, 4).copy(), q[1].copy(); c[:, e] = v[0].reshape(128, -1, 4); s[:, e] = v[1]
    return (c.reshape(128, -1), s)
def pk(c, s):
    return (np.ascontiguousarray(c), mx_ref.live(s))
def emit(q):
    return q[0], q[1]
def decode(q):
    o = []
    for b in range(4):
        e = np.zeros((128, 128, 4), np.float32); e[np.arange(128), np.arange(128), b] = 1
        o.append(mx_ref.matmul(mx_ref.quantize(e.reshape(128, 512).astype(BF)), q))
    return np.stack(o, axis=2).reshape(128, -1)
def f(rng, *shape):
    return mx_ref.flush((rng.standard_normal(shape, dtype=np.float32) * np.exp2(rng.integers(-2, 3, shape[:-1] + (1,)))).astype(BF))
def wide(rng, *shape, cols=0):
    v = rng.standard_normal(shape, dtype=np.float32) * np.exp2(rng.integers(-12, 13, shape)).astype(np.float32)
    if cols: v *= np.repeat(np.exp2(rng.integers(-cols, cols + 1, shape[:-2] + (1, shape[-1] // 4))) * (rng.random(shape[:-2] + (1, shape[-1] // 4)) > 0.0625), 4, axis=-1).astype(np.float32)
    return mx_ref.flush(v.astype(BF))
C, R, O = 192, 2, 2
def sized(v, k=1):
    v = np.asarray(v).astype(np.float32) * np.asarray(k, np.float32)
    v[np.abs(v) < np.float32(2.0 ** -8)] = 0
    return v.astype(BF)
def alike(t):
    return np.repeat(t[None], N, axis=0)
def setup_inputs(rng):
    k = np.exp2(rng.integers(1, 6, (N, 1, C)))
    return {"x": sized(f(rng, N, 128, 4 * C), np.repeat(k, 4, axis=2)), "b": alike(sized(f(rng, 128, 512), 8)), "w": f(rng, N, 128, 512 * O)}
def setup_inputs_ties(rng):
    d = setup_inputs(rng)
    x = np.stack([cols(d["x"][r], rng.permutation(C) % 24 - 1) for r in range(N)])
    z, e = int(rng.integers(0, N)), np.full(C, -1)
    e[int(rng.integers(0, C))] = 0
    x[z] = cols(d["x"][z], e)
    return {"x": x, "b": alike(cols(d["b"][0], rng.permutation(128) % 12 - 1)), "w": d["w"]}
def setup_inputs_near(rng):
    p = rng.choice([-1.0, 1.0], (128, 64, 4))
    k = np.sort(rng.permutation(128).reshape(64, 2), axis=1)
    b = np.zeros((128, 128, 4))
    b[:, k[:, 0]] = p
    b[:, k[:, 1]] = p
    b[:8] = 0
    b[120:] = 0
    b[127, k[:, 1], 3] = 1
    x = np.zeros((N, 128, C, 4))
    for r in range(N):
        v = 0.5 * rng.choice([-1.0, 1.0], (128, C, 4))
        j = np.sort(rng.permutation(C)[:128].reshape(64, 2), axis=1)
        v[:, j[:, 0]] = p
        v[:, j[:, 1]] = p
        v[120:] = 0
        v[127, j[:, 1], 3] = 2.0 ** -14
        x[r] = v * 2.0 ** int(rng.integers(8, 12))
    x[0, :8] = 2.0 ** 27
    x[1:N - 1, :8] = rng.choice([-1.0, 1.0], (N - 2, 8, C, 4)) * rng.integers(1, 16, (N - 2, 8, C, 4))
    x[N - 1, :8] = -2.0 ** 27
    return {"x": sized(x.reshape(N, 128, 4 * C)), "b": alike(sized(b.reshape(128, 512))), "w": f(rng, N, 128, 512 * O)}
def setup_inputs_low(rng):
    sign = np.ones(N)
    sign[rng.permutation(N)[:N // 4]] = -1
    def far(*shape):
        return (1 + rng.random(shape)) * np.exp2(rng.integers(28, 30, shape))
    return {"x": sized(far(N, 128, 4 * C), sign[:, None, None]), "b": alike(sized(far(128, 512), -1)), "w": f(rng, N, 128, 512 * O)}
def setup_inputs_lone(rng):
    q = rng.choice([-1.0, 1.0], (128, C, 4)) * rng.integers(4, 8, (128, C, 4))
    h = int(rng.integers(0, N))
    x = np.stack([q[:, rng.permutation(C)] * (16.0 if r == h else 1.0) for r in range(N)])
    b = sized(f(rng, 128, 4), 8).astype(np.float32)[:, None, :] * np.exp2(rng.integers(0, 6, (1, 128, 1)))
    return {"x": sized(x.reshape(N, 128, 4 * C)), "b": alike(sized(b.reshape(128, 512))), "w": f(rng, N, 128, 512 * O)}
def setup_inputs_spread(rng):
    return {"x": sized(wide(rng, N, 128, 4 * C, cols=6), 64), "b": alike(sized(wide(rng, 128, 512, cols=4), 64)), "w": f(rng, N, 128, 512 * O)}
def check_inputs(d):
    bad = []
    for k, low in (("x", 2.0 ** -8), ("b", 2.0 ** -30), ("w", 2.0 ** -30)):
        v = np.abs(d[k].astype(np.float32))
        if not (np.isfinite(v).all() and ((v == 0) | (v >= low) & (v <= 2.0 ** 30)).all()): bad.append("a value of " + k)
    v = d["b"].astype(np.float32)
    if (v != v[:1]).any(): bad.append("b differs between ranks")
    return bad
def match(g):
    g = g + np.float32(0)
    j, k = np.argmax(g, axis=1), np.argmax(g, axis=0)
    both = k[j] == np.arange(128)
    e = j.copy()
    e[~both] = np.setdiff1d(np.arange(C), j[both])[:np.sum(~both)]
    return e, both
def reference(x, b, w):
    T = [mx_ref.quantize(np.ascontiguousarray(x[r])) for r in range(N)]
    B = mx_ref.quantize(np.ascontiguousarray(b[0]))
    pa = np.zeros((N, R, 128), np.float32)
    for t in range(R):
        m = [match(mx_ref.matmul(B, T[r])) for r in range(N)]
        v = [decode(pick(T[r], m[r][0])) for r in range(N)]
        s = v[0]
        for r in range(1, N): s = s + v[r]
        B = mx_ref.quantize((s * np.float32(0.125)).astype(BF))
        d = decode(B)
        for r in range(N):
            e, both = m[r]
            pa[r, t] = e
            new = mx_ref.quantize(((v[r] + d) * np.float32(0.5)).astype(BF))
            T[r] = put(T[r], e[both], pick(new, np.flatnonzero(both)))
    y = np.zeros((N, 128, O * (C + 128)), np.float32)
    oc, osc = np.zeros((N, 128, 4 * C), np.uint8), np.zeros((N, 16, C), np.uint8)
    for r in range(N):
        for o in range(O):
            i = o * (C + 128)
            y[r, :, i:i + C + 128] = mx_ref.matmul(mx_ref.quantize(np.ascontiguousarray(cut(w[r], o))), join(T[r], B))
        oc[r], osc[r] = emit(T[r])
    return {"y": y, "oc": oc, "osc": osc, "pa": pa}

@@ -1,0 +1,350 @@
+from concourse.bass import DstId, RemoteDMATransfer
+from concourse.mybir import dt, AluOpType, ActivationFunctionType
+
+C, R, K, HALF = 192, 2, 128, 64
+F8, U8, BF, F32 = "float8_e4m3fn_x4", "uint8", "bfloat16", "float32"
+
+SCRATCH = {
+    "xs": ("sbuf", [128, 4 * C], BF), "bs": ("sbuf", [128, 512], BF), "ws": ("sbuf", [128, 1024], BF),
+    "hh": ("sbuf", [128, 4 * C], BF), "ones": ("sbuf", [128, 512], BF),
+    "he1": ("sbuf", [128, 768], BF), "he2": ("sbuf", [128, 1536], BF), "hx": ("sbuf", [128, 512], BF),
+    "ha": ("sbuf", [128, 512], BF), "hv": ("sbuf", [128, 512], BF),
+    "iok": ("sbuf", [128, K], BF), "eye": ("sbuf", [128, K], BF), "tri": ("sbuf", [128, K], BF),
+    "n16": ("sbuf", [128, C], BF), "mrow0": ("sbuf", [128, C], BF), "mrow": ("sbuf", [128, C], BF),
+    "jk0": ("sbuf", [128, C + K], F32), "jk": ("sbuf", [128, C + K], F32),
+    "cols": ("sbuf", [128, 8], F32), "pint": ("sbuf", [128, 2], "int32"), "best": ("sbuf", [128, 4], F32),
+    "pma": ("sbuf", [128, K], F32), "pmb": ("sbuf", [128, K], F32), "pmg": ("sbuf", [128, C + 1], F32),
+    "ja": ("sbuf", [128, K], BF), "jb": ("sbuf", [128, K], BF), "mg": ("sbuf", [128, C], BF), "mpm": ("sbuf", [128, C], BF),
+    "sc": ("sbuf", [128, C], F32), "sr": ("sbuf", [128, K], F32), "sr2": ("sbuf", [128, C], F32),
+    "val": ("sbuf", [128, K], F32), "win": ("sbuf", [128, R * C], F32), "win2": ("sbuf", [128, C], F32),
+    "par": ("sbuf", [128, R * K], F32), "ys": ("sbuf", [128, 2 * (C + K)], F32),
+}
+for _n, _w in (("tv0", C + K), ("tv1", C + K), ("tv2", C), ("bb0", K), ("bb1", 2 * K), ("bb2", 2 * K), ("p0", K), ("p1", K),
+               ("land0", 7 * HALF + K), ("land1", 7 * HALF + K), ("wq", 2 * K), ("eq", HALF + 4 * K), ("xq", K), ("oq", K),
+               ("q1", K), ("q2", C), ("q3", K)):
+    SCRATCH[_n] = ("sbuf", [128, _w], F8)
+    SCRATCH[_n + "s"] = ("sbuf", [128, _w], U8)
+for _t in range(R):
+    SCRATCH["offp%d" % _t] = ("sbuf", [128, K // 16], "uint16")
+    SCRATCH["offt%d" % _t] = ("sbuf", [128, C // 16], "uint16")
+for _i in range(8):
+    SCRATCH["ps%d" % _i] = ("psum", [128, 512], F32)
+
+NPOOL = 144
+SHARED = ["arr1", "arr20", "arr21", "sent"]
+SEMAPHORES = SHARED + ["s%d" % _i for _i in range(NPOOL)]
+
+STEP, RESET = 512.0, 16384.0
+FAR = -1e29
+
+
+def owners(t):
+    return [[4 * t, 4 * t + 1], [4 * t + 2, 4 * t + 3]]
+
+
+def rank_program(g, core, T, topo):
+    rank = T.rank_of(core)
+    if rank is None:
+        return
+    N = len(T.cores)
+    V, S, P, Y = g.vector, g.scalar, g.tensor, g.sync
+    A, ACT = AluOpType, ActivationFunctionType
+    names, count, seen, done = {n: n for n in SHARED}, {}, {}, {}
+
+    def sem(name):
+        if name not in names:
+            names[name] = "s%d" % (len(names) - len(SHARED))
+        return T.sem[names[name]]
+
+    def sig(ins, name, n=1):
+        ins.then_inc(sem(name), n)
+        count[name] = count.get(name, 0) + n
+
+    queues = {"V": V, "S": S, "P": P, "Y": Y, "G": g}
+
+    def wait(q, *ns):
+        for name in ns:
+            if seen.get((q, name), 0) < count[name]:
+                queues[q].wait_ge(sem(name), count[name])
+                seen[(q, name)] = count[name]
+                done[name] = count[name]
+
+    def mm(out, l, a, r, b, n, start=True, stop=True):
+        return P.matmul_mx(out[:, 0:n], T[l][:, a:a + K], T[l + "s"][:, a:a + K], T[r][:, b:b + n], T[r + "s"][:, b:b + n], start, stop)
+
+    def quant(q, a, n, tile):
+        return V.quantize_mx(T[q][:, a:a + n], T[q + "s"][:, a:a + n], tile)
+
+    def maskof(engs):
+        return sum(1 << e for e in engs)
+
+    def dst(r):
+        rid, pid = topo.addr(T.cores[r], core)
+        return DstId(rid=rid, pnc=pid)
+
+    def side(name, a, n, codes):
+        return T[name][:, a:a + n].bitcast(dt.uint8) if codes else T[name + "s"][:, a:a + n]
+
+    ps = [T["ps%d" % i] for i in range(8)]
+    EAT = [HALF + 3 * K, HALF, HALF + K, HALF + 2 * K]
+    pcol, tha, thb, off0, off1 = (T.cols[:, i:i + 1] for i in range(5))
+    engs = [e for e in topo.engines(core, T.cores[(rank + 1) % N]) if all(e in topo.engines(core, c) for c in T.cores if c != core)]
+    nh = len(engs) // 2
+
+    sig(Y.dma_start(T.xs[:], T.x[:]), "x", 16)
+    sig(S.dma_start(T.bs[:], T.b[:]), "b", 16)
+    wait("Y", "x")
+    sig(Y.dma_start(T.ws[:], T.w[:]), "w", 16)
+
+    fl = dict(allow_small_or_imprecise_dtypes=True)
+    sig(g.iota(pcol, [[0, 1]], 0, 1, **fl), "io1")
+    sig(g.iota(T.iok[:], [[1, K]], 0, 0, **fl), "io1")
+    sig(g.iota(T.pint[:, 0:1], [[0, 1]], 0, 1), "io2")
+    sig(g.iota(T.n16[:], [[0, C // 16], [-int(STEP), 16]], 15 * int(STEP), 0, **fl), "io3")
+    sig(g.iota(T.cols[0:HALF, 1:2], [[0, 1]], -1, -1, **fl), "tha")
+    sig(g.iota(thb, [[0, 1]], -1 - 2 * HALF, -2, **fl), "thb")
+    sig(g.iota(T.jk0[:], [[1, C + K]], 0, 0, **fl), "io4")
+
+    sig(V.memset(T.hh[:], 0.0), "hh0")
+    sig(V.memset(T.ones[:], 1.0), "ones")
+    sig(V.memset(T.pmg[:, 0:1], FAR), "ones")
+    sig(V.memset(T.cols[HALF:128, 1:2], -1e9), "tha")
+    wait("S", "hh0")
+    sig(S.activation(T.he1[:], T.hh[:], ACT.Copy), "he1z")
+    sig(S.activation(T.hx[:], T.hh[:, 0:512], ACT.Copy), "hxz")
+    wait("V", "io1")
+    sig(V.tensor_scalar(T.eye[:], T.iok[:], pcol, 128.0, A.is_equal, A.mult), "eye")
+    sig(V.tensor_scalar(T.tri[:], T.iok[:], pcol, None, A.is_lt), "eye")
+    wait("V", "io2")
+    sig(V.tensor_scalar(T.pint[:, 1:2], T.pint[:, 0:1], 15, None, A.bitwise_and), "p16")
+    wait("V", "he1z")
+    sig(V.tensor_scalar(T.he1[:, 0:4 * HALF:4], T.iok[:, 0:HALF], pcol, None, A.is_equal), "he1")
+    sig(V.tensor_scalar(T.he1[:, 4 * HALF + 1:768:4], T.iok[:], pcol, None, A.is_equal), "he1")
+    wait("V", "p16")
+    sig(V.tensor_scalar(off0, T.pint[:, 1:2], -STEP, 15 * STEP, A.mult, A.add), "off")
+    sig(V.tensor_scalar(off1, T.pint[:, 1:2], -STEP, 15 * STEP + 126.0, A.mult, A.add), "off")
+    wait("V", "he1")
+    sig(quant("eq", 0, C, T.he1[:]), "k1")
+    wait("V", "hxz", "eye")
+    sig(V.tensor_scalar(T.hx[:, 0:512:4], T.eye[:], -513.0 / 128.0, 1.0, A.mult, A.add), "hx")
+    sig(V.tensor_tensor(T.hx[:, 1:512:4], T.tri[:], T.eye[:], A.subtract), "hx")
+    wait("V", "x")
+    sig(quant("tv0", 0, C, T.xs[:]), "t0")
+    wait("V", "b")
+    sig(quant("bb0", 0, K, T.bs[:]), "t0")
+    wait("V", "hx")
+    sig(quant("xq", 0, K, T.hx[:]), "xq")
+    wait("V", "io3", "off", "ones")
+    sig(V.tensor_scalar(T.mrow0[:], T.n16[:], off0, RESET + STEP, A.is_equal, A.mult), "mrow0")
+
+    for t in range(R):
+        u = str(t)
+        tv, nxt, pk, land = "tv" + u, "tv%d" % (t + 1), "p" + u, "land" + u
+        bb, b0 = ("bb0", 0) if t == 0 else ("bb1", HALF)
+        nb = "bb%d" % (t + 1)
+        offp, offt = T["offp" + u], T["offt" + u]
+        own = owners(t)
+        half = [h for h in range(2) if rank in own[h]]
+        half = half[0] if half else None
+
+        wait("P", "t" + u)
+        sig(mm(ps[1], tv, 0, bb, b0, K), "ga" + u)
+        sig(mm(ps[2], tv, HALF, bb, b0, K), "gb" + u)
+        sig(mm(ps[0], bb, b0, tv, 0, C), "gg" + u)
+        wait("V", "ga" + u)
+        sig(V.tensor_tensor_scan(T.pma[:], ps[1][:, 0:K], T.ones[:, 0:K], FAR, A.max, A.mult), "sa" + u)
+        wait("V", "gb" + u)
+        sig(V.tensor_tensor_scan(T.pmb[:], ps[2][:, 0:K], T.ones[:, 0:K], FAR, A.max, A.mult), "sb" + u)
+        wait("V", "gg" + u)
+        sig(V.tensor_tensor_scan(T.pmg[:, 1:C + 1], ps[0][:, 0:C], T.ones[:, 0:C], FAR, A.max, A.mult), "sg" + u)
+        wait("S", "sa" + u)
+        sig(S.activation(T.ja[:], T.pma[:], ACT.Sign, bias=T.pma[:, K - 1:K], scale=-1.0, accum_out=T.best[:, 0:1]), "aa" + u)
+        wait("S", "sb" + u)
+        sig(S.activation(T.jb[:], T.pmb[:], ACT.Sign, bias=T.pmb[:, K - 1:K], scale=-1.0, accum_out=T.best[:, 1:2]), "ab" + u)
+        wait("S", "sg" + u)
+        sig(S.activation(T.mg[:], T.pmg[:, 0:C], ACT.Sign, bias=T.pmg[:, C:C + 1], scale=-1.0, accum_out=T.best[:, 2:3]), "ag" + u)
+        wait("S", "ag" + u)
+        sig(S.activation(T.mpm[:], T.mg[:], ACT.Identity, bias=-1.0, scale=2.0), "mp" + u)
+        if t == 0:
+            wait("S", "mrow0")
+            sig(S.activation(T.mrow[:], T.mrow0[:], ACT.Identity, bias=-STEP), "mrow")
+
+        wait("V", "aa" + u)
+        sig(V.tensor_scalar(T.hh[:, 0:512:4], T.iok[:], T.best[:, 0:1], None, A.is_equal), "oh" + u)
+        wait("V", "ab" + u)
+        sig(V.tensor_scalar(T.hh[:, 1:512:4], T.iok[:], T.best[:, 1:2], None, A.is_equal), "oh" + u)
+        wait("V", "oh" + u)
+        sig(quant("q1", 0, K, T.hh[:, 0:512]), "q1" + u)
+        if t == 0:
+            sig(quant("oq", 0, K, T.ones[:]), "oq")
+        wait("V", "ag" + u)
+        sig(V.tensor_scalar(T.best[:, 3:4], T.best[:, 2:3], 1.5 - C, None, A.add), "th" + u)
+        wait("P", "k1", "q1" + u)
+        sig(mm(ps[3], "q1", 0, "eq", 0, C), "cc" + u)
+        wait("V", "mp" + u, "th" + u, "cc" + u)
+        sig(V.tensor_tensor_scan(T.sc[:], T.mpm[:], ps[3][:, 0:C], 0.0, A.add, A.min), "sc" + u)
+
+        wait("V", "sc" + u)
+        sig(V.tensor_scalar(T.hh[:, 0:768:4], T.mpm[:], T.sc[:, C - 1:C], T.best[:, 3:4], A.add, A.is_gt), "h2" + u)
+        sig(V.tensor_scalar(T.hh[:, 1:768:4], T.ones[:, 0:C], T.sc[:, C - 1:C], T.best[:, 3:4], A.add, A.is_lt), "h2" + u)
+        wait("V", "h2" + u)
+        sig(quant("q2", 0, C, T.hh[:]), "q2" + u)
+        wait("P", "xq", "q2" + u)
+        sig(mm(ps[5], "q2", HALF, "xq", 0, K), "db" + u)
+        sig(mm(ps[4], "q2", 0, "xq", 0, K), "da" + u)
+        sig(mm(ps[7], "q2", 0, "eq", EAT[1], K), "un" + u)
+        wait("S", "thb", "db" + u)
+        sig(S.activation(T.hh[:, 1:512:4], ps[5][:, 0:K], ACT.Sign, bias=thb, scale=-2.0), "h3" + u)
+        wait("V", "tha", "da" + u)
+        sig(V.tensor_scalar(T.hh[:, 0:512:4], ps[4][:, 0:K], tha, 2.0, A.is_le, A.mult), "h3" + u)
+        if t == 0:
+            wait("S", "io4")
+            sig(S.activation(T.jk[:], T.jk0[:], ACT.Copy, scale=1.0 / STEP), "jk")
+
+        wait("V", "h3" + u)
+        sig(quant("q3", 0, K, T.hh[:, 0:512]), "q3" + u)
+        wait("P", "oq", "q3" + u)
+        sig(mm(ps[6], "oq", 0, "q3", 0, K), "ar" + u)
+        wait("V", "mrow", "ar" + u)
+        sig(V.tensor_tensor_scan(T.sr[:], T.mrow[:, 0:K], ps[6][:, 0:K], 0.0, A.add, A.min), "sr" + u)
+        wait("V", "sr" + u)
+        sig(V.tensor_scalar(offp[:], T.sr[:, 15:K:16], off1, 0.5, A.add, A.mult), "op" + u)
+        wait("V", "op" + u)
+        sig(V.tensor_copy(T[pk][:].bitcast(dt.uint32), T[tv][:, 0:C].bitcast(dt.uint32).indirect(offp[:])), "pc" + u)
+        wait("S", "op" + u)
+        sig(S.activation(T[pk + "s"][:], T[tv + "s"][:, 0:C].indirect(offp[:]), ACT.Copy), "psc" + u)
+
+        for codes in (True, False):
+            wait("G", ("pc" if codes else "psc") + u)
+            trs = []
+            for h in range(2):
+                to = [o for o in own[h] if o != rank]
+                trs.append(RemoteDMATransfer(
+                    dst_ids=[dst(o) for o in to], dma_engine_mask=maskof(engs[nh * h:nh * h + nh]), remote_sem=T.sem.arr1,
+                    srcs=[side(pk, HALF * h, HALF, codes)],
+                    dsts=[side(land, K * h + HALF * (rank - (rank > o)), HALF, codes) for o in to]))
+            g.remote_dma_fused(trs, local_sem=sem("sent"))
+            count["sent"] = count.get("sent", 0) + 2 * nh
+
+        sig(S.activation(T.par[0:1, K * t:K * t + K], ps[6][0:1, 0:K], ACT.Identity, bias=63.0, scale=0.5), "pa" + u)
+        wait("Y", "pa" + u)
+        sig(Y.dma_start(T.pa[t:t + 1, :], T.par[0:1, K * t:K * t + K]), "outy", 16)
+        wait("V", "jk", "un" + u)
+        sig(V.tensor_tensor(T.val[:], T.jk[:, C:C + K], ps[7][:, 0:K], A.subtract), "val" + u)
+        if t == 0:
+            sig(V.memset(T.he2[:], 0.0), "he2z")
+            sig(V.memset(T.ha[:], 0.0), "haz")
+            wait("V", "he2z")
+            for b in (2, 3, 0):
+                a = 4 * (EAT[b] - C)
+                sig(V.tensor_scalar(T.he2[:, a + b:a + 512:4], T.iok[:], pcol, None, A.is_equal), "he2")
+            wait("V", "he2")
+            sig(quant("eq", C, 3 * K, T.he2[:]), "e")
+        if half is not None:
+            sig(quant(land, 7 * HALF if half == 0 else 0, K, T.ones[:]), "pad")
+        wait("P", "e", "pc" + u, "psc" + u)
+        for b in range(4):
+            mm(ps[b], "eq", EAT[b], pk, 0, K, True, False)
+        wait("P", "pa" + u, "val" + u)
+
+        if half is not None:
+            count["arr1"] = (N - 1) * 2 * nh
+            wait("P", "pad", "arr1")
+            for b in range(4):
+                for r in range(N):
+                    src, a = (pk, 0) if r == rank else (land, HALF * half + HALF * (r - (r > rank)))
+                    ins = mm(ps[4 + b], "eq", EAT[b], src, a, K, r == 0, r == N - 1)
+                sig(ins, "sum%d" % b)
+            for b in range(4):
+                o = T.ha[:, 256 * (1 - half) + b:256 * (2 - half):4]
+                i = ps[4 + b][:, HALF * half:HALF * half + HALF]
+                q = "S" if b % 2 == 0 else "V"
+                wait(q, "haz", "sum%d" % b)
+                if q == "S":
+                    sig(S.activation(o, i, ACT.Copy, scale=1.0 / N), "ha")
+                else:
+                    sig(V.tensor_scalar(o, i, 1.0 / N, None, A.mult), "ha")
+            wait("V", "ha")
+            sig(quant(nb, K * half, K, T.ha[:]), "qa")
+            i = own[half].index(rank)
+            rest = [r for r in range(N) if r not in own[0] + own[1]]
+            to = [rest[2 * i], rest[2 * i + 1], own[1 - half][i]]
+            wait("G", "qa")
+            for codes in (True, False):
+                v = side(nb, HALF + HALF * half, HALF, codes)
+                g.remote_dma_fused([RemoteDMATransfer(dst_ids=[dst(r) for r in to], dma_engine_mask=maskof(engs),
+                                                      remote_sem=T.sem["arr2" + u], srcs=[v], dsts=[v for r in to])],
+                                   local_sem=sem("sent"))
+                count["sent"] += 2 * nh
+
+        if t == 0:
+            sig(V.memset(T.win[:], -1.0), "winz")
+        wait("V", "winz", "val" + u)
+        sig(V.tensor_copy(T.win[:, C * t:C * t + C].indirect(offp[:]), T.val[:]), "sct" + u)
+        wait("V", "sct" + u)
+        sig(V.tensor_tensor(T.win2[:], T.win[:, C * t:C * t + C], T.jk[:, 0:C], A.max), "w2" + u)
+        wait("V", "w2" + u)
+        sig(V.tensor_tensor_scan(T.sr2[:], T.mrow[:], T.win2[:], 0.0, A.add, A.min), "st" + u)
+        wait("V", "st" + u)
+        sig(V.tensor_scalar(offt[:], T.sr2[:, 15:C:16], off0, STEP, A.add, A.mult), "ot" + u)
+        if t == 0:
+            wait("V", "w")
+            sig(quant("wq", 0, 2 * K, T.ws[:]), "wq")
+
+        count["arr2" + u] = (2 if half is None else 1) * 4 * nh
+        if half is not None:
+            wait("P", "qa")
+        wait("P", "arr2" + u)
+        for b in range(4):
+            sig(mm(ps[b], "eq", EAT[b], nb, HALF, K, False, True), "dv%d" % b + u)
+        last = t == R - 1
+        if last:
+            wait("P", "wq")
+            for o in range(2):
+                sig(mm(ps[4 + o], "wq", K * o, nb, HALF, K), "yb%d" % o)
+        for b in range(4):
+            q = "S" if b % 2 == 0 else "V"
+            wait(q, "dv%d" % b + u)
+            if q == "S":
+                sig(S.activation(T.hv[:, b:512:4], ps[b][:, 0:K], ACT.Copy, scale=0.5), "hv" + u)
+            else:
+                sig(V.tensor_scalar(T.hv[:, b:512:4], ps[b][:, 0:K], 0.5, None, A.mult), "hv" + u)
+        wait("V", "hv" + u, "ot" + u)
+        sig(quant(tv, C, K, T.hv[:]), "qv" + u)
+        if last:
+            wait("S", "yb0")
+            sig(S.activation(T.ys[:, C:C + K], ps[4][:, 0:K], ACT.Copy), "cb0")
+        nx = "t%d" % (t + 1)
+        wait("V", "qv" + u)
+        sig(V.tensor_copy(T[nxt][:, 0:C].bitcast(dt.uint32), T[tv][:].bitcast(dt.uint32).indirect(offt[:])), nx)
+        wait("S", "ot" + u, "qv" + u)
+        sig(S.activation(T[nxt + "s"][:, 0:C], T[tv + "s"][:].indirect(offt[:]), ACT.Copy), nx)
+
+    W = C + K
+    wait("Y", "cb0")
+    sig(Y.dma_start(T.y[:, C:W], T.ys[:, C:W]), "outy", 16)
+    wait("S", "yb1")
+    sig(S.activation(T.ys[:, W + C:2 * W], ps[5][:, 0:K], ACT.Copy), "cy1")
+    wait("P", "t2")
+    for o in range(2):
+        sig(mm(ps[6 + o], "wq", K * o, "tv2", 0, C), "yt%d" % o)
+    wait("Y", "t2")
+    sig(Y.dma_start(T.oc[:], T.tv2[:].bitcast(dt.uint8)), "outy", 16)
+    wait("V", "yt0")
+    sig(V.tensor_copy(T.ys[:, 0:C], ps[6][:, 0:C]), "cy0")
+    wait("S", "yt1")
+    sig(S.activation(T.ys[:, W:W + C], ps[7][:, 0:C], ACT.Copy), "cy1")
+    for k in range(2):
+        sig(Y.dma_start(T.osc[4 * k:4 * k + 4, :], T.tv2s[32 * k:32 * k + 4, :]), "outy", 16)
+    wait("Y", "cy0")
+    sig(Y.dma_start(T.y[:, 0:C], T.ys[:, 0:C]), "outy", 16)
+    wait("S", "cy1")
+    sig(S.dma_start(T.y[:, W:2 * W], T.ys[:, W:2 * W]), "outs", 16)
+    wait("S", "t2")
+    for k in range(2, 4):
+        sig(S.dma_start(T.osc[4 * k:4 * k + 4, :], T.tv2s[32 * k:32 * k + 4, :]), "outs", 16)
+    wait("Y", "outy")
+    wait("S", "outs")
+    for name in list(count):
+        if done.get(name, 0) < count[name]:
+            wait("G", name)

@@ -1,27 +1,29 @@
 from concourse.bass import DstId, RemoteDMATransfer
 from concourse.mybir import dt, AluOpType, ActivationFunctionType
 
-C, R, K, HALF = 192, 2, 128, 64
+C, R, K, HALF, NR = 192, 2, 128, 64, 8
+AW = NR * HALF
 F8, U8, BF, F32 = "float8_e4m3fn_x4", "uint8", "bfloat16", "float32"
 
 SCRATCH = {
     "xs": ("sbuf", [128, 4 * C], BF), "bs": ("sbuf", [128, 512], BF), "ws": ("sbuf", [128, 1024], BF),
-    "hh": ("sbuf", [128, 4 * C], BF), "ones": ("sbuf", [128, 512], BF),
-    "he1": ("sbuf", [128, 768], BF), "he2": ("sbuf", [128, 1536], BF), "hx": ("sbuf", [128, 512], BF),
-    "ha": ("sbuf", [128, 512], BF), "hv": ("sbuf", [128, 512], BF),
-    "iok": ("sbuf", [128, K], BF), "eye": ("sbuf", [128, K], BF), "tri": ("sbuf", [128, K], BF),
+    "hh": ("sbuf", [128, 512], BF), "hw": ("sbuf", [128, 832], BF), "cx": ("sbuf", [128, 2 * K], BF),
+    "h1": ("sbuf", [128, 512], BF), "ones": ("sbuf", [128, 520], BF),
+    "he1": ("sbuf", [128, 832], BF), "hz": ("sbuf", [128, 520], BF), "hz8": ("sbuf", [128, 520], BF),
+    "hx": ("sbuf", [128, 512], BF), "ha": ("sbuf", [128, 512], BF), "hv": ("sbuf", [128, 512], BF),
+    "iok": ("sbuf", [128, K], BF), "tri": ("sbuf", [128, K], BF), "ntri": ("sbuf", [128, K], BF),
     "n16": ("sbuf", [128, C], BF), "mrow0": ("sbuf", [128, C], BF), "mrow": ("sbuf", [128, C], BF),
+    "acc": ("sbuf", [128, 2 * AW], F32),
     "jk0": ("sbuf", [128, C + K], F32), "jk": ("sbuf", [128, C + K], F32),
-    "cols": ("sbuf", [128, 8], F32), "pint": ("sbuf", [128, 2], "int32"), "best": ("sbuf", [128, 4], F32),
-    "pma": ("sbuf", [128, K], F32), "pmb": ("sbuf", [128, K], F32), "pmg": ("sbuf", [128, C + 1], F32),
-    "ja": ("sbuf", [128, K], BF), "jb": ("sbuf", [128, K], BF), "mg": ("sbuf", [128, C], BF), "mpm": ("sbuf", [128, C], BF),
-    "sc": ("sbuf", [128, C], F32), "sr": ("sbuf", [128, K], F32), "sr2": ("sbuf", [128, C], F32),
+    "cols": ("sbuf", [128, 8], F32), "pint": ("sbuf", [128, 2], "int32"), "best": ("sbuf", [128, 2], F32),
+    "pma": ("sbuf", [128, K + 1], F32), "pmb": ("sbuf", [128, K + 1], F32), "pmg": ("sbuf", [128, C + 1], F32),
+    "sc": ("sbuf", [128, C + 1], F32), "sr": ("sbuf", [128, K], F32), "sr2": ("sbuf", [128, C], F32),
     "val": ("sbuf", [128, K], F32), "win": ("sbuf", [128, R * C], F32), "win2": ("sbuf", [128, C], F32),
     "par": ("sbuf", [128, R * K], F32), "ys": ("sbuf", [128, 2 * (C + K)], F32),
 }
 for _n, _w in (("tv0", C + K), ("tv1", C + K), ("tv2", C), ("bb0", K), ("bb1", 2 * K), ("bb2", 2 * K), ("p0", K), ("p1", K),
-               ("land0", 7 * HALF + K), ("land1", 7 * HALF + K), ("wq", 2 * K), ("eq", HALF + 4 * K), ("xq", K), ("oq", K),
-               ("q1", K), ("q2", C), ("q3", K)):
+               ("land0", K + AW), ("land1", K + AW), ("wq", 2 * K), ("e1", C + 2), ("uq", K),
+               ("eq", 4 * K), ("e8", 2 * K), ("xq", K), ("oq", K), ("q1", K), ("q2", C), ("q3", K)):
     SCRATCH[_n] = ("sbuf", [128, _w], F8)
     SCRATCH[_n + "s"] = ("sbuf", [128, _w], U8)
 for _t in range(R):
@@ -30,9 +32,8 @@ for _t in range(R):
 for _i in range(8):
     SCRATCH["ps%d" % _i] = ("psum", [128, 512], F32)
 
-NPOOL = 144
-SHARED = ["arr1", "arr20", "arr21", "sent"]
-SEMAPHORES = SHARED + ["s%d" % _i for _i in range(NPOOL)]
+SHARED = ["sent", "lo", "hi", "arr0", "arr1"]
+SEMAPHORES = SHARED + ["s%d" % _i for _i in range(150 - len(SHARED))]
 
 STEP, RESET = 512.0, 16384.0
 FAR = -1e29
@@ -75,6 +76,12 @@ def rank_program(g, core, T, topo):
     def quant(q, a, n, tile):
         return V.quantize_mx(T[q][:, a:a + n], T[q + "s"][:, a:a + n], tile)
 
+    def pickc(to, a, n, src, w, off):
+        return V.tensor_copy(T[to][:, a:a + n].bitcast(dt.uint32), T[src][:, 0:w].bitcast(dt.uint32).indirect(off))
+
+    def picks(to, a, n, src, w, off):
+        return S.activation(T[to + "s"][:, a:a + n], T[src + "s"][:, 0:w].indirect(off), ACT.Copy)
+
     def maskof(engs):
         return sum(1 << e for e in engs)
 
@@ -85,14 +92,18 @@ def rank_program(g, core, T, topo):
     def side(name, a, n, codes):
         return T[name][:, a:a + n].bitcast(dt.uint8) if codes else T[name + "s"][:, a:a + n]
 
+    def unpacker(b):
+        return quant("eq", K * b, K, T.hz[:, 3 - b:515 - b])
+
     ps = [T["ps%d" % i] for i in range(8)]
-    EAT = [HALF + 3 * K, HALF, HALF + K, HALF + 2 * K]
     pcol, tha, thb, off0, off1 = (T.cols[:, i:i + 1] for i in range(5))
     engs = [e for e in topo.engines(core, T.cores[(rank + 1) % N]) if all(e in topo.engines(core, c) for c in T.cores if c != core)]
     nh = len(engs) // 2
+    count["sent"] = 0
+    W = C + K
 
-    sig(Y.dma_start(T.xs[:], T.x[:]), "x", 16)
     sig(S.dma_start(T.bs[:], T.b[:]), "b", 16)
+    sig(Y.dma_start(T.xs[:], T.x[:]), "x", 16)
     wait("Y", "x")
     sig(Y.dma_start(T.ws[:], T.w[:]), "w", 16)
 
@@ -101,41 +112,49 @@ def rank_program(g, core, T, topo):
     sig(g.iota(T.iok[:], [[1, K]], 0, 0, **fl), "io1")
     sig(g.iota(T.pint[:, 0:1], [[0, 1]], 0, 1), "io2")
     sig(g.iota(T.n16[:], [[0, C // 16], [-int(STEP), 16]], 15 * int(STEP), 0, **fl), "io3")
-    sig(g.iota(T.cols[0:HALF, 1:2], [[0, 1]], -1, -1, **fl), "tha")
-    sig(g.iota(thb, [[0, 1]], -1 - 2 * HALF, -2, **fl), "thb")
-    sig(g.iota(T.jk0[:], [[1, C + K]], 0, 0, **fl), "io4")
 
-    sig(V.memset(T.hh[:], 0.0), "hh0")
+    sig(V.memset(T.hw[:], 1.0), "hw1")
     sig(V.memset(T.ones[:], 1.0), "ones")
-    sig(V.memset(T.pmg[:, 0:1], FAR), "ones")
+    for pm in (T.pma, T.pmb, T.pmg):
+        sig(V.memset(pm[:, 0:1], FAR), "far")
     sig(V.memset(T.cols[HALF:128, 1:2], -1e9), "tha")
-    wait("S", "hh0")
-    sig(S.activation(T.he1[:], T.hh[:], ACT.Copy), "he1z")
-    sig(S.activation(T.hx[:], T.hh[:, 0:512], ACT.Copy), "hxz")
+    wait("S", "hw1")
+    sig(S.activation(T.he1[:], T.hw[:], ACT.Copy, scale=0.0), "he1z")
+    wait("S", "ones")
+    sig(S.activation(T.hx[:], T.ones[:, 0:512], ACT.Copy, scale=0.0), "hxz")
+    sig(S.activation(T.h1[:], T.ones[:, 0:512], ACT.Copy, scale=0.5), "h1c")
+    sig(S.activation(T.hh[:], T.ones[:, 0:512], ACT.Copy, scale=0.0), "hhz")
     wait("V", "io1")
-    sig(V.tensor_scalar(T.eye[:], T.iok[:], pcol, 128.0, A.is_equal, A.mult), "eye")
-    sig(V.tensor_scalar(T.tri[:], T.iok[:], pcol, None, A.is_lt), "eye")
+    sig(V.tensor_scalar(T.tri[:], T.iok[:], pcol, None, A.is_lt), "tri")
+    sig(V.tensor_scalar(T.ntri[:], T.iok[:], pcol, -1.0, A.is_lt, A.mult), "tri")
     wait("V", "io2")
     sig(V.tensor_scalar(T.pint[:, 1:2], T.pint[:, 0:1], 15, None, A.bitwise_and), "p16")
+    wait("V", "b")
+    sig(quant("bb0", 0, K, T.bs[:]), "t0")
     wait("V", "he1z")
-    sig(V.tensor_scalar(T.he1[:, 0:4 * HALF:4], T.iok[:, 0:HALF], pcol, None, A.is_equal), "he1")
-    sig(V.tensor_scalar(T.he1[:, 4 * HALF + 1:768:4], T.iok[:], pcol, None, A.is_equal), "he1")
+    for s in range(2):
+        sig(V.tensor_scalar(T.he1[0:HALF, s:4 * HALF:4], T.iok[0:HALF, 0:HALF], T.cols[0:HALF, 0:1], 0.5 - s, A.is_equal, A.mult), "he1")
+        sig(V.tensor_scalar(T.he1[:, 4 * HALF + 2 + s:768:4], T.iok[:], pcol, 0.5 - s, A.is_equal, A.mult), "he1")
+    wait("G", "io1", "io2", "io3", "he1z")
+    sig(g.iota(T.he1[HALF:HALF + 1, 0:832:4], [[16, C // 16 + 1], [0, 16]], 0, 0, **fl), "he1g")
+    wait("G", "he1g")
+    wait("V", "io3")
+    sig(V.tensor_scalar(T.he1[96:97, 0:768:4], T.n16[96:97, :], -1.0 / STEP, 15.0, A.mult, A.add), "he1")
     wait("V", "p16")
     sig(V.tensor_scalar(off0, T.pint[:, 1:2], -STEP, 15 * STEP, A.mult, A.add), "off")
     sig(V.tensor_scalar(off1, T.pint[:, 1:2], -STEP, 15 * STEP + 126.0, A.mult, A.add), "off")
-    wait("V", "he1")
-    sig(quant("eq", 0, C, T.he1[:]), "k1")
-    wait("V", "hxz", "eye")
-    sig(V.tensor_scalar(T.hx[:, 0:512:4], T.eye[:], -513.0 / 128.0, 1.0, A.mult, A.add), "hx")
-    sig(V.tensor_tensor(T.hx[:, 1:512:4], T.tri[:], T.eye[:], A.subtract), "hx")
     wait("V", "x")
     sig(quant("tv0", 0, C, T.xs[:]), "t0")
-    wait("V", "b")
-    sig(quant("bb0", 0, K, T.bs[:]), "t0")
-    wait("V", "hx")
-    sig(quant("xq", 0, K, T.hx[:]), "xq")
-    wait("V", "io3", "off", "ones")
-    sig(V.tensor_scalar(T.mrow0[:], T.n16[:], off0, RESET + STEP, A.is_equal, A.mult), "mrow0")
+    wait("V", "he1", "he1g")
+    sig(quant("e1", 0, C + 2, T.he1[:, 0:4 * C + 8]), "k1")
+    count["u0"] = 0
+    wait("G", "hxz", "tri", "ones")
+    sig(g.affine_select(T.hx[:, 1:512:4], T.tri[:], [[-1, K]], A.not_equal, -128.0, 0, 1), "hx")
+    sig(g.affine_select(T.cx[:, 0:2 * K:2], T.ones[:, 0:K], [[-1, K]], A.not_equal, -512.0, 0, 1), "hx")
+    sig(g.affine_select(T.cx[:, 1:2 * K:2], T.ntri[:], [[-1, K]], A.not_equal, 128.0, 0, 1), "hx")
+    sig(g.iota(T.cols[0:HALF, 1:2], [[0, 1]], -1, -1, **fl), "tha")
+    sig(g.iota(thb, [[0, 1]], -1 - 2 * HALF, -2, **fl), "thb")
+    sig(g.affine_select(T.hz[:], T.ones[:], [[-1, 520]], A.is_equal, 0.0, 3, 4), "hz")
 
     for t in range(R):
         u = str(t)
@@ -146,201 +165,236 @@ def rank_program(g, core, T, topo):
         own = owners(t)
         half = [h for h in range(2) if rank in own[h]]
         half = half[0] if half else None
+        last = t == R - 1
 
         wait("P", "t" + u)
-        sig(mm(ps[1], tv, 0, bb, b0, K), "ga" + u)
-        sig(mm(ps[2], tv, HALF, bb, b0, K), "gb" + u)
-        sig(mm(ps[0], bb, b0, tv, 0, C), "gg" + u)
-        wait("V", "ga" + u)
-        sig(V.tensor_tensor_scan(T.pma[:], ps[1][:, 0:K], T.ones[:, 0:K], FAR, A.max, A.mult), "sa" + u)
-        wait("V", "gb" + u)
-        sig(V.tensor_tensor_scan(T.pmb[:], ps[2][:, 0:K], T.ones[:, 0:K], FAR, A.max, A.mult), "sb" + u)
-        wait("V", "gg" + u)
-        sig(V.tensor_tensor_scan(T.pmg[:, 1:C + 1], ps[0][:, 0:C], T.ones[:, 0:C], FAR, A.max, A.mult), "sg" + u)
-        wait("S", "sa" + u)
-        sig(S.activation(T.ja[:], T.pma[:], ACT.Sign, bias=T.pma[:, K - 1:K], scale=-1.0, accum_out=T.best[:, 0:1]), "aa" + u)
-        wait("S", "sb" + u)
-        sig(S.activation(T.jb[:], T.pmb[:], ACT.Sign, bias=T.pmb[:, K - 1:K], scale=-1.0, accum_out=T.best[:, 1:2]), "ab" + u)
-        wait("S", "sg" + u)
-        sig(S.activation(T.mg[:], T.pmg[:, 0:C], ACT.Sign, bias=T.pmg[:, C:C + 1], scale=-1.0, accum_out=T.best[:, 2:3]), "ag" + u)
-        wait("S", "ag" + u)
-        sig(S.activation(T.mpm[:], T.mg[:], ACT.Identity, bias=-1.0, scale=2.0), "mp" + u)
+        sig(mm(ps[1], tv, 0, bb, b0, K), "ga")
+        wait("P", "u" + u)
+        sig(mm(ps[2], tv, HALF, bb, b0, K), "gb")
+        sig(mm(ps[0], bb, b0, tv, 0, C), "gg")
+        wait("V", "far", "ga")
+        sig(V.tensor_tensor_scan(T.pma[:, 1:K + 1], ps[1][:, 0:K], T.ones[:, 0:K], FAR, A.max, A.mult), "sa")
+        wait("V", "gb")
+        sig(V.tensor_tensor_scan(T.pmb[:, 1:K + 1], ps[2][:, 0:K], T.ones[:, 0:K], FAR, A.max, A.mult), "sb")
+        wait("V", "gg")
+        sig(V.tensor_tensor_scan(T.pmg[:, 1:C + 1], ps[0][:, 0:C], T.ones[:, 0:C], FAR, A.max, A.mult), "sg")
+
+        wait("S", "h1c", "sa")
+        for s in range(2):
+            sig(S.activation(T.h1[0:HALF, s:512:4], T.pma[0:HALF, s:K + s], ACT.Sign, bias=T.pma[0:HALF, K:K + 1], scale=-1.0), "oh")
+        wait("S", "sb")
+        sig(S.activation(T.h1[:, 3:512:4], T.pmb[:, 1:K + 1], ACT.Sign, bias=T.pmb[:, K:K + 1], scale=-1.0), "oh")
+        wait("S", "he1z", "sg")
+        sig(S.activation(T.hw[:, 0:4 * C:4], T.pmg[:, 0:C], ACT.Sign, bias=T.pmg[:, C:C + 1], scale=-1.0, accum_out=T.best[:, 0:1]), "ag")
+        wait("V", "h1c", "sb")
+        sig(V.tensor_scalar(T.h1[:, 2:512:4], T.pmb[:, 0:K], T.pmb[:, K:K + 1], None, A.is_lt), "oh")
+        wait("V", "oh")
+        sig(quant("q1", 0, K, T.h1[:]), "q1")
+        wait("V", "ag")
+        sig(V.tensor_scalar(T.hw[:, 4 * C:4 * C + 1], T.best[:, 0:1], -0.5, 0.5, A.mult, A.add), "th")
+        sig(quant("q2", 0, C, T.hw[:, 0:4 * C]), "q2")
+        wait("P", "k1", "q1")
+        sig(mm(ps[3], "q1", 0, "e1", 0, C + 2), "cc")
+        wait("V", "th", "cc")
+        sig(V.tensor_tensor_scan(T.sc[:], T.hw[:, 0:4 * C + 4:4], ps[3][:, 0:C + 1], 0.0, A.add, A.min), "sc")
+
+        mut = T.sc[:, C:C + 1]
+        wait("V", "hx", "sc")
+        sig(V.tensor_scalar(T.hx[:, 0:512:2], T.cx[:], mut, 2.0, A.mult, A.mult), "h2")
+        wait("V", "h2")
+        sig(quant("xq", 0, K, T.hx[:]), "xq")
+        if t == 0:
+            wait("V", "off")
+            sig(V.tensor_scalar(T.mrow0[:], T.n16[:], off0, RESET + STEP, A.is_equal, A.mult), "mrow0")
+            sig(quant("oq", 0, K, T.ones[:, 0:512]), "oq")
+        wait("P", "xq", "q2")
+        sig(mm(ps[5], "q2", HALF, "xq", 0, K), "db")
+        sig(mm(ps[4], "q2", 0, "xq", 0, K), "da")
+        wait("S", "hhz", "thb", "db")
+        sig(S.activation(T.hh[:, 1:512:4], ps[5][:, 0:K], ACT.Sign, bias=thb, scale=-2.0), "h3")
+        wait("V", "hhz", "tha", "da")
+        sig(V.tensor_scalar(T.hh[:, 0:512:4], ps[4][:, 0:K], tha, 2.0, A.is_le, A.mult), "h3")
         if t == 0:
             wait("S", "mrow0")
             sig(S.activation(T.mrow[:], T.mrow0[:], ACT.Identity, bias=-STEP), "mrow")
 
-        wait("V", "aa" + u)
-        sig(V.tensor_scalar(T.hh[:, 0:512:4], T.iok[:], T.best[:, 0:1], None, A.is_equal), "oh" + u)
-        wait("V", "ab" + u)
-        sig(V.tensor_scalar(T.hh[:, 1:512:4], T.iok[:], T.best[:, 1:2], None, A.is_equal), "oh" + u)
-        wait("V", "oh" + u)
-        sig(quant("q1", 0, K, T.hh[:, 0:512]), "q1" + u)
-        if t == 0:
-            sig(quant("oq", 0, K, T.ones[:]), "oq")
-        wait("V", "ag" + u)
-        sig(V.tensor_scalar(T.best[:, 3:4], T.best[:, 2:3], 1.5 - C, None, A.add), "th" + u)
-        wait("P", "k1", "q1" + u)
-        sig(mm(ps[3], "q1", 0, "eq", 0, C), "cc" + u)
-        wait("V", "mp" + u, "th" + u, "cc" + u)
-        sig(V.tensor_tensor_scan(T.sc[:], T.mpm[:], ps[3][:, 0:C], 0.0, A.add, A.min), "sc" + u)
-
-        wait("V", "sc" + u)
-        sig(V.tensor_scalar(T.hh[:, 0:768:4], T.mpm[:], T.sc[:, C - 1:C], T.best[:, 3:4], A.add, A.is_gt), "h2" + u)
-        sig(V.tensor_scalar(T.hh[:, 1:768:4], T.ones[:, 0:C], T.sc[:, C - 1:C], T.best[:, 3:4], A.add, A.is_lt), "h2" + u)
-        wait("V", "h2" + u)
-        sig(quant("q2", 0, C, T.hh[:]), "q2" + u)
-        wait("P", "xq", "q2" + u)
-        sig(mm(ps[5], "q2", HALF, "xq", 0, K), "db" + u)
-        sig(mm(ps[4], "q2", 0, "xq", 0, K), "da" + u)
-        sig(mm(ps[7], "q2", 0, "eq", EAT[1], K), "un" + u)
-        wait("S", "thb", "db" + u)
-        sig(S.activation(T.hh[:, 1:512:4], ps[5][:, 0:K], ACT.Sign, bias=thb, scale=-2.0), "h3" + u)
-        wait("V", "tha", "da" + u)
-        sig(V.tensor_scalar(T.hh[:, 0:512:4], ps[4][:, 0:K], tha, 2.0, A.is_le, A.mult), "h3" + u)
-        if t == 0:
-            wait("S", "io4")
-            sig(S.activation(T.jk[:], T.jk0[:], ACT.Copy, scale=1.0 / STEP), "jk")
-
-        wait("V", "h3" + u)
-        sig(quant("q3", 0, K, T.hh[:, 0:512]), "q3" + u)
-        wait("P", "oq", "q3" + u)
-        sig(mm(ps[6], "oq", 0, "q3", 0, K), "ar" + u)
-        wait("V", "mrow", "ar" + u)
-        sig(V.tensor_tensor_scan(T.sr[:], T.mrow[:, 0:K], ps[6][:, 0:K], 0.0, A.add, A.min), "sr" + u)
-        wait("V", "sr" + u)
-        sig(V.tensor_scalar(offp[:], T.sr[:, 15:K:16], off1, 0.5, A.add, A.mult), "op" + u)
-        wait("V", "op" + u)
-        sig(V.tensor_copy(T[pk][:].bitcast(dt.uint32), T[tv][:, 0:C].bitcast(dt.uint32).indirect(offp[:])), "pc" + u)
-        wait("S", "op" + u)
-        sig(S.activation(T[pk + "s"][:], T[tv + "s"][:, 0:C].indirect(offp[:]), ACT.Copy), "psc" + u)
+        wait("V", "h3")
+        sig(quant("q3", 0, K, T.hh[:]), "q3")
+        wait("P", "oq", "q3")
+        sig(mm(ps[6], "oq", 0, "q3", 0, K), "ar")
+        wait("V", "mrow", "ar")
+        sig(V.tensor_tensor_scan(T.sr[:], T.mrow[:, 0:K], ps[6][:, 0:K], 0.0, A.add, A.min), "sr")
+        wait("V", "sr")
+        sig(V.tensor_scalar(offp[:], T.sr[:, 15:K:16], off1, 0.5, A.add, A.mult), "op")
+        wait("V", "op")
+        sig(pickc(pk, 0, K, tv, C, offp[:]), "pc")
+        wait("S", "op")
+        sig(picks(pk, 0, K, tv, C, offp[:]), "psc")
 
         for codes in (True, False):
-            wait("G", ("pc" if codes else "psc") + u)
+            wait("G", "pc" if codes else "psc")
             trs = []
             for h in range(2):
                 to = [o for o in own[h] if o != rank]
+                e = h if codes else 1 - h
                 trs.append(RemoteDMATransfer(
-                    dst_ids=[dst(o) for o in to], dma_engine_mask=maskof(engs[nh * h:nh * h + nh]), remote_sem=T.sem.arr1,
-                    srcs=[side(pk, HALF * h, HALF, codes)],
-                    dsts=[side(land, K * h + HALF * (rank - (rank > o)), HALF, codes) for o in to]))
+                    dst_ids=[dst(o) for o in to], dma_engine_mask=maskof(engs[nh * e:nh * e + nh]),
+                    remote_sem=T.sem["lo" if rank < N // 2 else "hi"], srcs=[side(pk, HALF * h, HALF, codes)],
+                    dsts=[side(land, K + HALF * rank, HALF, codes) for o in to]))
             g.remote_dma_fused(trs, local_sem=sem("sent"))
-            count["sent"] = count.get("sent", 0) + 2 * nh
+            count["sent"] += 2 * nh
 
+        if half is not None:
+            mine = offp[:, 4 * half:4 * half + 4]
+            sig(pickc(land, K + HALF * rank, HALF, tv, C, mine), "oc")
+            sig(picks(land, K + HALF * rank, HALF, tv, C, mine), "oc")
+        wait("S", "sr")
         sig(S.activation(T.par[0:1, K * t:K * t + K], ps[6][0:1, 0:K], ACT.Identity, bias=63.0, scale=0.5), "pa" + u)
         wait("Y", "pa" + u)
         sig(Y.dma_start(T.pa[t:t + 1, :], T.par[0:1, K * t:K * t + K]), "outy", 16)
-        wait("V", "jk", "un" + u)
-        sig(V.tensor_tensor(T.val[:], T.jk[:, C:C + K], ps[7][:, 0:K], A.subtract), "val" + u)
+        if half is not None:
+            wait("S", "hz")
+            sig(S.activation(T.hz8[:], T.hz[:], ACT.Copy, scale=1.0 / N), "hz8")
+        wait("V", "hz")
+        sig(V.tensor_scalar(T.hh[:, 0:512:4], T.hz[:, 3:515:4], mut, 2.0, A.mult, A.mult), "hu")
+        sig(V.memset(T.hh[:, 1:512:4], 0.0), "hu")
         if t == 0:
-            sig(V.memset(T.he2[:], 0.0), "he2z")
-            sig(V.memset(T.ha[:], 0.0), "haz")
-            wait("V", "he2z")
-            for b in (2, 3, 0):
-                a = 4 * (EAT[b] - C)
-                sig(V.tensor_scalar(T.he2[:, a + b:a + 512:4], T.iok[:], pcol, None, A.is_equal), "he2")
-            wait("V", "he2")
-            sig(quant("eq", C, 3 * K, T.he2[:]), "e")
+            sig(g.iota(T.jk0[:], [[1, C + K]], 0, 0, **fl), "io4")
+            sig(S.activation(T.win[:], T.ones[:, 0:R * C], ACT.Copy, scale=-1.0), "winz")
+            wait("S", "io4")
+            sig(S.activation(T.jk[:, 0:C], T.jk0[:, 0:C], ACT.Copy, scale=1.0 / STEP), "jk")
+            sig(S.activation(T.jk[:, C:W], T.jk0[:, C:W], ACT.Identity, bias=-1.0, scale=1.0 / STEP), "jk")
+            sig(unpacker(0), "e")
+        wait("V", "hu")
+        sig(quant("uq", 0, K, T.hh[:]), "uq")
+        wait("P", "uq")
+        sig(mm(ps[7], "oq", 0, "uq", 0, K), "un")
+        if t == 0:
+            for b in (1, 2, 3):
+                sig(unpacker(b), "e")
         if half is not None:
-            sig(quant(land, 7 * HALF if half == 0 else 0, K, T.ones[:]), "pad")
-        wait("P", "e", "pc" + u, "psc" + u)
-        for b in range(4):
-            mm(ps[b], "eq", EAT[b], pk, 0, K, True, False)
-        wait("P", "pa" + u, "val" + u)
+            sig(S.activation(T.ha[:], T.ones[:, 0:512], ACT.Copy), "haz")
+            sig(quant(land, 0, K, T.ones[:, 0:512]), "pad")
+            wait("V", "hz8")
+            for b in range(2):
+                sig(quant("e8", K * b, K, T.hz8[:, 3 - b:515 - b]), "pad")
+        if last:
+            wait("V", "w")
+            sig(quant("wq", 0, 2 * K, T.ws[:]), "wq")
+        wait("V", "jk", "un")
+        sig(V.tensor_tensor(T.val[:], T.jk[:, C:W], ps[7][:, 0:K], A.add), "val")
+        wait("V", "winz", "val")
+        sig(V.tensor_copy(T.win[:, C * t:C * t + C].indirect(offp[:]), T.val[:]), "sct")
 
+        wait("P", "e")
         if half is not None:
-            count["arr1"] = (N - 1) * 2 * nh
-            wait("P", "pad", "arr1")
-            for b in range(4):
-                for r in range(N):
-                    src, a = (pk, 0) if r == rank else (land, HALF * half + HALF * (r - (r > rank)))
-                    ins = mm(ps[4 + b], "eq", EAT[b], src, a, K, r == 0, r == N - 1)
-                sig(ins, "sum%d" % b)
-            for b in range(4):
-                o = T.ha[:, 256 * (1 - half) + b:256 * (2 - half):4]
-                i = ps[4 + b][:, HALF * half:HALF * half + HALF]
-                q = "S" if b % 2 == 0 else "V"
-                wait(q, "haz", "sum%d" % b)
-                if q == "S":
-                    sig(S.activation(o, i, ACT.Copy, scale=1.0 / N), "ha")
-                else:
-                    sig(V.tensor_scalar(o, i, 1.0 / N, None, A.mult), "ha")
+            a = 256 * (1 - half)
+            for part, name in enumerate(("lo", "hi")):
+                rs = range(4 * part, 4 * part + 4)
+                count[name] = 2 * nh * len([r for r in rs if r != rank])
+                wait("P", "pad", "oc", name)
+                for b in range(2):
+                    sig(mm(ps[2 * part + b], "e8", K * b, land, K + 4 * HALF * part, 4 * HALF), "un%d%d" % (part, b))
+                for b in (2, 3):
+                    for r in rs:
+                        ins = mm(ps[2 + b], "eq", K * b, land, HALF + HALF * r, K, r == 0, r == N - 1)
+                    if part == 1:
+                        sig(ins, "sum%d" % b)
+                for r in rs:
+                    for b in range(2):
+                        o = T.acc[:, AW * b + HALF * r:AW * b + HALF * r + HALF]
+                        i = ps[2 * part + b][:, HALF * (r % 4):HALF * (r % 4) + HALF]
+                        wait("V", "un%d%d" % (part, b))
+                        if r == 0:
+                            sig(V.tensor_copy(o, i), "ad%d" % b)
+                            continue
+                        wait("V", "haz", "ad%d" % b)
+                        if r == N - 1:
+                            o = T.ha[:, a + b:a + 256:4]
+                        sig(V.tensor_tensor(o, T.acc[:, AW * b + HALF * (r - 1):AW * b + HALF * r], i, A.add),
+                            "ad%d" % b if r < N - 1 else "ha")
+            for b in (2, 3):
+                wait("S", "haz", "sum%d" % b)
+                sig(S.activation(T.ha[:, a + b:a + 256:4], ps[2 + b][:, HALF:K], ACT.Copy, scale=1.0 / N), "ha")
             wait("V", "ha")
             sig(quant(nb, K * half, K, T.ha[:]), "qa")
             i = own[half].index(rank)
             rest = [r for r in range(N) if r not in own[0] + own[1]]
-            to = [rest[2 * i], rest[2 * i + 1], own[1 - half][i]]
+            other = [own[1 - half][i]]
             wait("G", "qa")
-            for codes in (True, False):
-                v = side(nb, HALF + HALF * half, HALF, codes)
-                g.remote_dma_fused([RemoteDMATransfer(dst_ids=[dst(r) for r in to], dma_engine_mask=maskof(engs),
-                                                      remote_sem=T.sem["arr2" + u], srcs=[v], dsts=[v for r in to])],
-                                   local_sem=sem("sent"))
-                count["sent"] += 2 * nh
+            for to in ([rest[2 * i:2 * i + 2] + other] if last else [other, rest[2 * i:2 * i + 2]]):
+                for codes in (True, False):
+                    v = side(nb, HALF + HALF * half, HALF, codes)
+                    g.remote_dma_fused([RemoteDMATransfer(dst_ids=[dst(r) for r in to], dma_engine_mask=maskof(engs),
+                                                          remote_sem=T.sem["arr" + u], srcs=[v], dsts=[v for r in to])],
+                                       local_sem=sem("sent"))
+                    count["sent"] += 2 * nh
+            wait("P", "ha")
 
-        if t == 0:
-            sig(V.memset(T.win[:], -1.0), "winz")
-        wait("V", "winz", "val" + u)
-        sig(V.tensor_copy(T.win[:, C * t:C * t + C].indirect(offp[:]), T.val[:]), "sct" + u)
-        wait("V", "sct" + u)
-        sig(V.tensor_tensor(T.win2[:], T.win[:, C * t:C * t + C], T.jk[:, 0:C], A.max), "w2" + u)
-        wait("V", "w2" + u)
-        sig(V.tensor_tensor_scan(T.sr2[:], T.mrow[:], T.win2[:], 0.0, A.add, A.min), "st" + u)
-        wait("V", "st" + u)
-        sig(V.tensor_scalar(offt[:], T.sr2[:, 15:C:16], off0, STEP, A.add, A.mult), "ot" + u)
-        if t == 0:
-            wait("V", "w")
-            sig(quant("wq", 0, 2 * K, T.ws[:]), "wq")
+        wait("P", "pc", "psc", "pa" + u, "val")
+        for b in range(4):
+            mm(ps[b], "eq", K * b, pk, 0, K, True, False)
+        wait("V", "sct")
+        sig(V.tensor_tensor(T.win2[:], T.win[:, C * t:C * t + C], T.jk[:, 0:C], A.max), "w2")
+        wait("V", "w2")
+        sig(V.tensor_tensor_scan(T.sr2[:], T.mrow[:], T.win2[:], 0.0, A.add, A.min), "st")
+        wait("V", "st")
+        sig(V.tensor_scalar(offt[:], T.sr2[:, 15:C:16], off0, STEP, A.add, A.mult), "ot")
 
-        count["arr2" + u] = (2 if half is None else 1) * 4 * nh
+        count["arr" + u] = (2 if half is None else 1) * 4 * nh
         if half is not None:
             wait("P", "qa")
-        wait("P", "arr2" + u)
+        wait("P", "arr" + u)
         for b in range(4):
-            sig(mm(ps[b], "eq", EAT[b], nb, HALF, K, False, True), "dv%d" % b + u)
-        last = t == R - 1
+            sig(mm(ps[b], "eq", K * b, nb, HALF, K, False, True), "dv%d" % b)
         if last:
             wait("P", "wq")
             for o in range(2):
                 sig(mm(ps[4 + o], "wq", K * o, nb, HALF, K), "yb%d" % o)
         for b in range(4):
             q = "S" if b % 2 == 0 else "V"
-            wait(q, "dv%d" % b + u)
+            wait(q, "dv%d" % b)
             if q == "S":
-                sig(S.activation(T.hv[:, b:512:4], ps[b][:, 0:K], ACT.Copy, scale=0.5), "hv" + u)
+                sig(S.activation(T.hv[:, b:512:4], ps[b][:, 0:K], ACT.Copy, scale=0.5), "hv")
             else:
-                sig(V.tensor_scalar(T.hv[:, b:512:4], ps[b][:, 0:K], 0.5, None, A.mult), "hv" + u)
-        wait("V", "hv" + u, "ot" + u)
-        sig(quant(tv, C, K, T.hv[:]), "qv" + u)
+                sig(V.tensor_scalar(T.hv[:, b:512:4], ps[b][:, 0:K], 0.5, None, A.mult), "hv")
+        wait("V", "hv", "ot")
+        sig(quant(tv, C, K, T.hv[:]), "qv")
         if last:
-            wait("S", "yb0")
-            sig(S.activation(T.ys[:, C:C + K], ps[4][:, 0:K], ACT.Copy), "cb0")
-        nx = "t%d" % (t + 1)
-        wait("V", "qv" + u)
-        sig(V.tensor_copy(T[nxt][:, 0:C].bitcast(dt.uint32), T[tv][:].bitcast(dt.uint32).indirect(offt[:])), nx)
-        wait("S", "ot" + u, "qv" + u)
-        sig(S.activation(T[nxt + "s"][:, 0:C], T[tv + "s"][:].indirect(offt[:]), ACT.Copy), nx)
+            for o in range(2):
+                wait("S", "yb%d" % o)
+                sig(S.activation(T.ys[:, W * o + C:W * o + W], ps[4 + o][:, 0:K], ACT.Copy), "cb%d" % o)
+                wait("Y", "cb%d" % o)
+                sig(Y.dma_start(T.y[:, W * o + C:W * o + W], T.ys[:, W * o + C:W * o + W]), "outy", 16)
+        wait("V", "qv")
+        wait("S", "ot", "qv")
+        for a, n, nx in ((0, K, "t%d" % (t + 1)), (K, C - K, "u%d" % (t + 1))):
+            sig(pickc(nxt, a, n, tv, W, offt[:, a // 16:(a + n) // 16]), nx)
+            sig(picks(nxt, a, n, tv, W, offt[:, a // 16:(a + n) // 16]), nx)
 
-    W = C + K
-    wait("Y", "cb0")
-    sig(Y.dma_start(T.y[:, C:W], T.ys[:, C:W]), "outy", 16)
-    wait("S", "yb1")
-    sig(S.activation(T.ys[:, W + C:2 * W], ps[5][:, 0:K], ACT.Copy), "cy1")
     wait("P", "t2")
     for o in range(2):
-        sig(mm(ps[6 + o], "wq", K * o, "tv2", 0, C), "yt%d" % o)
-    wait("Y", "t2")
+        sig(mm(ps[o], "wq", K * o, "tv2", 0, K), "yt%d" % o)
+    wait("P", "u2")
+    for o in range(2):
+        sig(mm(ps[2 + o], "wq", K * o, "tv2", HALF, K), "yu%d" % o)
+    wait("Y", "t2", "u2")
     sig(Y.dma_start(T.oc[:], T.tv2[:].bitcast(dt.uint8)), "outy", 16)
-    wait("V", "yt0")
-    sig(V.tensor_copy(T.ys[:, 0:C], ps[6][:, 0:C]), "cy0")
-    wait("S", "yt1")
-    sig(S.activation(T.ys[:, W:W + C], ps[7][:, 0:C], ACT.Copy), "cy1")
     for k in range(2):
         sig(Y.dma_start(T.osc[4 * k:4 * k + 4, :], T.tv2s[32 * k:32 * k + 4, :]), "outy", 16)
+    wait("V", "yt0")
+    sig(V.tensor_copy(T.ys[:, 0:K], ps[0][:, 0:K]), "cy0")
+    wait("V", "yu0")
+    sig(V.tensor_copy(T.ys[:, K:C], ps[2][:, HALF:K]), "cy0")
+    wait("S", "yt1")
+    sig(S.activation(T.ys[:, W:W + K], ps[1][:, 0:K], ACT.Copy), "cy1")
+    wait("S", "yu1")
+    sig(S.activation(T.ys[:, W + K:W + C], ps[3][:, HALF:K], ACT.Copy), "cy1")
     wait("Y", "cy0")
     sig(Y.dma_start(T.y[:, 0:C], T.ys[:, 0:C]), "outy", 16)
     wait("S", "cy1")
-    sig(S.dma_start(T.y[:, W:2 * W], T.ys[:, W:2 * W]), "outs", 16)
-    wait("S", "t2")
+    sig(S.dma_start(T.y[:, W:W + C], T.ys[:, W:W + C]), "outs", 16)
+    wait("S", "t2", "u2")
     for k in range(2, 4):
         sig(S.dma_start(T.osc[4 * k:4 * k + 4, :], T.tv2s[32 * k:32 * k + 4, :]), "outs", 16)
     wait("Y", "outy")

from concourse.bass import DstId, RemoteDMATransfer
from concourse.mybir import dt, AluOpType, ActivationFunctionType

C, R, K, HALF, NR = 192, 2, 128, 64, 8
AW = NR * HALF
F8, U8, BF, F32 = "float8_e4m3fn_x4", "uint8", "bfloat16", "float32"

SCRATCH = {
    "xs": ("sbuf", [128, 4 * C], BF), "bs": ("sbuf", [128, 512], BF), "ws": ("sbuf", [128, 1024], BF),
    "hh": ("sbuf", [128, 512], BF), "hw": ("sbuf", [128, 832], BF), "cx": ("sbuf", [128, 2 * K], BF),
    "h1": ("sbuf", [128, 512], BF), "ones": ("sbuf", [128, 520], BF),
    "he1": ("sbuf", [128, 832], BF), "hz": ("sbuf", [128, 520], BF), "hz8": ("sbuf", [128, 520], BF),
    "hx": ("sbuf", [128, 512], BF), "ha": ("sbuf", [128, 512], BF), "hv": ("sbuf", [128, 512], BF),
    "iok": ("sbuf", [128, K], BF), "tri": ("sbuf", [128, K], BF), "ntri": ("sbuf", [128, K], BF),
    "n16": ("sbuf", [128, C], BF), "mrow0": ("sbuf", [128, C], BF), "mrow": ("sbuf", [128, C], BF),
    "acc": ("sbuf", [128, 2 * AW], F32),
    "jk0": ("sbuf", [128, C + K], F32), "jk": ("sbuf", [128, C + K], F32),
    "cols": ("sbuf", [128, 8], F32), "pint": ("sbuf", [128, 2], "int32"), "best": ("sbuf", [128, 2], F32),
    "pma": ("sbuf", [128, K + 1], F32), "pmb": ("sbuf", [128, K + 1], F32), "pmg": ("sbuf", [128, C + 1], F32),
    "sc": ("sbuf", [128, C + 1], F32), "sr": ("sbuf", [128, K], F32), "sr2": ("sbuf", [128, C], F32),
    "val": ("sbuf", [128, K], F32), "win": ("sbuf", [128, R * C], F32), "win2": ("sbuf", [128, C], F32),
    "par": ("sbuf", [128, R * K], F32), "ys": ("sbuf", [128, 2 * (C + K)], F32),
}
for _n, _w in (("tv0", C + K), ("tv1", C + K), ("tv2", C), ("bb0", K), ("bb1", 2 * K), ("bb2", 2 * K), ("p0", K), ("p1", K),
               ("land0", K + AW), ("land1", K + AW), ("wq", 2 * K), ("e1", C + 2), ("uq", K),
               ("eq", 4 * K), ("e8", 2 * K), ("xq", K), ("oq", K), ("q1", K), ("q2", C), ("q3", K)):
    SCRATCH[_n] = ("sbuf", [128, _w], F8)
    SCRATCH[_n + "s"] = ("sbuf", [128, _w], U8)
for _t in range(R):
    SCRATCH["offp%d" % _t] = ("sbuf", [128, K // 16], "uint16")
    SCRATCH["offt%d" % _t] = ("sbuf", [128, C // 16], "uint16")
for _i in range(8):
    SCRATCH["ps%d" % _i] = ("psum", [128, 512], F32)

SHARED = ["sent", "lo", "hi", "arr0", "arr1"]
SEMAPHORES = SHARED + ["s%d" % _i for _i in range(150 - len(SHARED))]

STEP, RESET = 512.0, 16384.0
FAR = -1e29


def owners(t):
    return [[4 * t, 4 * t + 1], [4 * t + 2, 4 * t + 3]]


def rank_program(g, core, T, topo):
    rank = T.rank_of(core)
    if rank is None:
        return
    N = len(T.cores)
    V, S, P, Y = g.vector, g.scalar, g.tensor, g.sync
    A, ACT = AluOpType, ActivationFunctionType
    names, count, seen, done = {n: n for n in SHARED}, {}, {}, {}

    def sem(name):
        if name not in names:
            names[name] = "s%d" % (len(names) - len(SHARED))
        return T.sem[names[name]]

    def sig(ins, name, n=1):
        ins.then_inc(sem(name), n)
        count[name] = count.get(name, 0) + n

    queues = {"V": V, "S": S, "P": P, "Y": Y, "G": g}

    def wait(q, *ns):
        for name in ns:
            if seen.get((q, name), 0) < count[name]:
                queues[q].wait_ge(sem(name), count[name])
                seen[(q, name)] = count[name]
                done[name] = count[name]

    def mm(out, l, a, r, b, n, start=True, stop=True):
        return P.matmul_mx(out[:, 0:n], T[l][:, a:a + K], T[l + "s"][:, a:a + K], T[r][:, b:b + n], T[r + "s"][:, b:b + n], start, stop)

    def quant(q, a, n, tile):
        return V.quantize_mx(T[q][:, a:a + n], T[q + "s"][:, a:a + n], tile)

    def pickc(to, a, n, src, w, off):
        return V.tensor_copy(T[to][:, a:a + n].bitcast(dt.uint32), T[src][:, 0:w].bitcast(dt.uint32).indirect(off))

    def picks(to, a, n, src, w, off):
        return S.activation(T[to + "s"][:, a:a + n], T[src + "s"][:, 0:w].indirect(off), ACT.Copy)

    def maskof(engs):
        return sum(1 << e for e in engs)

    def dst(r):
        rid, pid = topo.addr(T.cores[r], core)
        return DstId(rid=rid, pnc=pid)

    def side(name, a, n, codes):
        return T[name][:, a:a + n].bitcast(dt.uint8) if codes else T[name + "s"][:, a:a + n]

    def unpacker(b):
        return quant("eq", K * b, K, T.hz[:, 3 - b:515 - b])

    ps = [T["ps%d" % i] for i in range(8)]
    pcol, tha, thb, off0, off1 = (T.cols[:, i:i + 1] for i in range(5))
    engs = [e for e in topo.engines(core, T.cores[(rank + 1) % N]) if all(e in topo.engines(core, c) for c in T.cores if c != core)]
    nh = len(engs) // 2
    count["sent"] = 0
    W = C + K

    sig(S.dma_start(T.bs[:], T.b[:]), "b", 16)
    sig(Y.dma_start(T.xs[:], T.x[:]), "x", 16)
    wait("Y", "x")
    sig(Y.dma_start(T.ws[:], T.w[:]), "w", 16)

    fl = dict(allow_small_or_imprecise_dtypes=True)
    sig(g.iota(pcol, [[0, 1]], 0, 1, **fl), "io1")
    sig(g.iota(T.iok[:], [[1, K]], 0, 0, **fl), "io1")
    sig(g.iota(T.pint[:, 0:1], [[0, 1]], 0, 1), "io2")
    sig(g.iota(T.n16[:], [[0, C // 16], [-int(STEP), 16]], 15 * int(STEP), 0, **fl), "io3")

    sig(V.memset(T.hw[:], 1.0), "hw1")
    sig(V.memset(T.ones[:], 1.0), "ones")
    for pm in (T.pma, T.pmb, T.pmg):
        sig(V.memset(pm[:, 0:1], FAR), "far")
    sig(V.memset(T.cols[HALF:128, 1:2], -1e9), "tha")
    wait("S", "hw1")
    sig(S.activation(T.he1[:], T.hw[:], ACT.Copy, scale=0.0), "he1z")
    wait("S", "ones")
    sig(S.activation(T.hx[:], T.ones[:, 0:512], ACT.Copy, scale=0.0), "hxz")
    sig(S.activation(T.h1[:], T.ones[:, 0:512], ACT.Copy, scale=0.5), "h1c")
    sig(S.activation(T.hh[:], T.ones[:, 0:512], ACT.Copy, scale=0.0), "hhz")
    wait("V", "io1")
    sig(V.tensor_scalar(T.tri[:], T.iok[:], pcol, None, A.is_lt), "tri")
    sig(V.tensor_scalar(T.ntri[:], T.iok[:], pcol, -1.0, A.is_lt, A.mult), "tri")
    wait("V", "io2")
    sig(V.tensor_scalar(T.pint[:, 1:2], T.pint[:, 0:1], 15, None, A.bitwise_and), "p16")
    wait("V", "b")
    sig(quant("bb0", 0, K, T.bs[:]), "t0")
    wait("V", "he1z")
    for s in range(2):
        sig(V.tensor_scalar(T.he1[0:HALF, s:4 * HALF:4], T.iok[0:HALF, 0:HALF], T.cols[0:HALF, 0:1], 0.5 - s, A.is_equal, A.mult), "he1")
        sig(V.tensor_scalar(T.he1[:, 4 * HALF + 2 + s:768:4], T.iok[:], pcol, 0.5 - s, A.is_equal, A.mult), "he1")
    wait("G", "io1", "io2", "io3", "he1z")
    sig(g.iota(T.he1[HALF:HALF + 1, 0:832:4], [[16, C // 16 + 1], [0, 16]], 0, 0, **fl), "he1g")
    wait("G", "he1g")
    wait("V", "io3")
    sig(V.tensor_scalar(T.he1[96:97, 0:768:4], T.n16[96:97, :], -1.0 / STEP, 15.0, A.mult, A.add), "he1")
    wait("V", "p16")
    sig(V.tensor_scalar(off0, T.pint[:, 1:2], -STEP, 15 * STEP, A.mult, A.add), "off")
    sig(V.tensor_scalar(off1, T.pint[:, 1:2], -STEP, 15 * STEP + 126.0, A.mult, A.add), "off")
    wait("V", "x")
    sig(quant("tv0", 0, C, T.xs[:]), "t0")
    wait("V", "he1", "he1g")
    sig(quant("e1", 0, C + 2, T.he1[:, 0:4 * C + 8]), "k1")
    count["u0"] = 0
    wait("G", "hxz", "tri", "ones")
    sig(g.affine_select(T.hx[:, 1:512:4], T.tri[:], [[-1, K]], A.not_equal, -128.0, 0, 1), "hx")
    sig(g.affine_select(T.cx[:, 0:2 * K:2], T.ones[:, 0:K], [[-1, K]], A.not_equal, -512.0, 0, 1), "hx")
    sig(g.affine_select(T.cx[:, 1:2 * K:2], T.ntri[:], [[-1, K]], A.not_equal, 128.0, 0, 1), "hx")
    sig(g.iota(T.cols[0:HALF, 1:2], [[0, 1]], -1, -1, **fl), "tha")
    sig(g.iota(thb, [[0, 1]], -1 - 2 * HALF, -2, **fl), "thb")
    sig(g.affine_select(T.hz[:], T.ones[:], [[-1, 520]], A.is_equal, 0.0, 3, 4), "hz")

    for t in range(R):
        u = str(t)
        tv, nxt, pk, land = "tv" + u, "tv%d" % (t + 1), "p" + u, "land" + u
        bb, b0 = ("bb0", 0) if t == 0 else ("bb1", HALF)
        nb = "bb%d" % (t + 1)
        offp, offt = T["offp" + u], T["offt" + u]
        own = owners(t)
        half = [h for h in range(2) if rank in own[h]]
        half = half[0] if half else None
        last = t == R - 1

        wait("P", "t" + u)
        sig(mm(ps[1], tv, 0, bb, b0, K), "ga")
        wait("P", "u" + u)
        sig(mm(ps[2], tv, HALF, bb, b0, K), "gb")
        sig(mm(ps[0], bb, b0, tv, 0, C), "gg")
        wait("V", "far", "ga")
        sig(V.tensor_tensor_scan(T.pma[:, 1:K + 1], ps[1][:, 0:K], T.ones[:, 0:K], FAR, A.max, A.mult), "sa")
        wait("V", "gb")
        sig(V.tensor_tensor_scan(T.pmb[:, 1:K + 1], ps[2][:, 0:K], T.ones[:, 0:K], FAR, A.max, A.mult), "sb")
        wait("V", "gg")
        sig(V.tensor_tensor_scan(T.pmg[:, 1:C + 1], ps[0][:, 0:C], T.ones[:, 0:C], FAR, A.max, A.mult), "sg")

        wait("S", "h1c", "sa")
        for s in range(2):
            sig(S.activation(T.h1[0:HALF, s:512:4], T.pma[0:HALF, s:K + s], ACT.Sign, bias=T.pma[0:HALF, K:K + 1], scale=-1.0), "oh")
        wait("S", "sb")
        sig(S.activation(T.h1[:, 3:512:4], T.pmb[:, 1:K + 1], ACT.Sign, bias=T.pmb[:, K:K + 1], scale=-1.0), "oh")
        wait("S", "he1z", "sg")
        sig(S.activation(T.hw[:, 0:4 * C:4], T.pmg[:, 0:C], ACT.Sign, bias=T.pmg[:, C:C + 1], scale=-1.0, accum_out=T.best[:, 0:1]), "ag")
        wait("V", "h1c", "sb")
        sig(V.tensor_scalar(T.h1[:, 2:512:4], T.pmb[:, 0:K], T.pmb[:, K:K + 1], None, A.is_lt), "oh")
        wait("V", "oh")
        sig(quant("q1", 0, K, T.h1[:]), "q1")
        wait("V", "ag")
        sig(V.tensor_scalar(T.hw[:, 4 * C:4 * C + 1], T.best[:, 0:1], -0.5, 0.5, A.mult, A.add), "th")
        sig(quant("q2", 0, C, T.hw[:, 0:4 * C]), "q2")
        wait("P", "k1", "q1")
        sig(mm(ps[3], "q1", 0, "e1", 0, C + 2), "cc")
        wait("V", "th", "cc")
        sig(V.tensor_tensor_scan(T.sc[:], T.hw[:, 0:4 * C + 4:4], ps[3][:, 0:C + 1], 0.0, A.add, A.min), "sc")

        mut = T.sc[:, C:C + 1]
        wait("V", "hx", "sc")
        sig(V.tensor_scalar(T.hx[:, 0:512:2], T.cx[:], mut, 2.0, A.mult, A.mult), "h2")
        wait("V", "h2")
        sig(quant("xq", 0, K, T.hx[:]), "xq")
        if t == 0:
            wait("V", "off")
            sig(V.tensor_scalar(T.mrow0[:], T.n16[:], off0, RESET + STEP, A.is_equal, A.mult), "mrow0")
            sig(quant("oq", 0, K, T.ones[:, 0:512]), "oq")
        wait("P", "xq", "q2")
        sig(mm(ps[5], "q2", HALF, "xq", 0, K), "db")
        sig(mm(ps[4], "q2", 0, "xq", 0, K), "da")
        wait("S", "hhz", "thb", "db")
        sig(S.activation(T.hh[:, 1:512:4], ps[5][:, 0:K], ACT.Sign, bias=thb, scale=-2.0), "h3")
        wait("V", "hhz", "tha", "da")
        sig(V.tensor_scalar(T.hh[:, 0:512:4], ps[4][:, 0:K], tha, 2.0, A.is_le, A.mult), "h3")
        if t == 0:
            wait("S", "mrow0")
            sig(S.activation(T.mrow[:], T.mrow0[:], ACT.Identity, bias=-STEP), "mrow")

        wait("V", "h3")
        sig(quant("q3", 0, K, T.hh[:]), "q3")
        wait("P", "oq", "q3")
        sig(mm(ps[6], "oq", 0, "q3", 0, K), "ar")
        wait("V", "mrow", "ar")
        sig(V.tensor_tensor_scan(T.sr[:], T.mrow[:, 0:K], ps[6][:, 0:K], 0.0, A.add, A.min), "sr")
        wait("V", "sr")
        sig(V.tensor_scalar(offp[:], T.sr[:, 15:K:16], off1, 0.5, A.add, A.mult), "op")
        wait("V", "op")
        sig(pickc(pk, 0, K, tv, C, offp[:]), "pc")
        wait("S", "op")
        sig(picks(pk, 0, K, tv, C, offp[:]), "psc")

        for codes in (True, False):
            wait("G", "pc" if codes else "psc")
            trs = []
            for h in range(2):
                to = [o for o in own[h] if o != rank]
                e = h if codes else 1 - h
                trs.append(RemoteDMATransfer(
                    dst_ids=[dst(o) for o in to], dma_engine_mask=maskof(engs[nh * e:nh * e + nh]),
                    remote_sem=T.sem["lo" if rank < N // 2 else "hi"], srcs=[side(pk, HALF * h, HALF, codes)],
                    dsts=[side(land, K + HALF * rank, HALF, codes) for o in to]))
            g.remote_dma_fused(trs, local_sem=sem("sent"))
            count["sent"] += 2 * nh

        if half is not None:
            mine = offp[:, 4 * half:4 * half + 4]
            sig(pickc(land, K + HALF * rank, HALF, tv, C, mine), "oc")
            sig(picks(land, K + HALF * rank, HALF, tv, C, mine), "oc")
        wait("S", "sr")
        sig(S.activation(T.par[0:1, K * t:K * t + K], ps[6][0:1, 0:K], ACT.Identity, bias=63.0, scale=0.5), "pa" + u)
        wait("Y", "pa" + u)
        sig(Y.dma_start(T.pa[t:t + 1, :], T.par[0:1, K * t:K * t + K]), "outy", 16)
        if half is not None:
            wait("S", "hz")
            sig(S.activation(T.hz8[:], T.hz[:], ACT.Copy, scale=1.0 / N), "hz8")
        wait("V", "hz")
        sig(V.tensor_scalar(T.hh[:, 0:512:4], T.hz[:, 3:515:4], mut, 2.0, A.mult, A.mult), "hu")
        sig(V.memset(T.hh[:, 1:512:4], 0.0), "hu")
        if t == 0:
            sig(g.iota(T.jk0[:], [[1, C + K]], 0, 0, **fl), "io4")
            sig(S.activation(T.win[:], T.ones[:, 0:R * C], ACT.Copy, scale=-1.0), "winz")
            wait("S", "io4")
            sig(S.activation(T.jk[:, 0:C], T.jk0[:, 0:C], ACT.Copy, scale=1.0 / STEP), "jk")
            sig(S.activation(T.jk[:, C:W], T.jk0[:, C:W], ACT.Identity, bias=-1.0, scale=1.0 / STEP), "jk")
            sig(unpacker(0), "e")
        wait("V", "hu")
        sig(quant("uq", 0, K, T.hh[:]), "uq")
        wait("P", "uq")
        sig(mm(ps[7], "oq", 0, "uq", 0, K), "un")
        if t == 0:
            for b in (1, 2, 3):
                sig(unpacker(b), "e")
        if half is not None:
            sig(S.activation(T.ha[:], T.ones[:, 0:512], ACT.Copy), "haz")
            sig(quant(land, 0, K, T.ones[:, 0:512]), "pad")
            wait("V", "hz8")
            for b in range(2):
                sig(quant("e8", K * b, K, T.hz8[:, 3 - b:515 - b]), "pad")
        if last:
            wait("V", "w")
            sig(quant("wq", 0, 2 * K, T.ws[:]), "wq")
        wait("V", "jk", "un")
        sig(V.tensor_tensor(T.val[:], T.jk[:, C:W], ps[7][:, 0:K], A.add), "val")
        wait("V", "winz", "val")
        sig(V.tensor_copy(T.win[:, C * t:C * t + C].indirect(offp[:]), T.val[:]), "sct")

        wait("P", "e")
        if half is not None:
            a = 256 * (1 - half)
            for part, name in enumerate(("lo", "hi")):
                rs = range(4 * part, 4 * part + 4)
                count[name] = 2 * nh * len([r for r in rs if r != rank])
                wait("P", "pad", "oc", name)
                for b in range(2):
                    sig(mm(ps[2 * part + b], "e8", K * b, land, K + 4 * HALF * part, 4 * HALF), "un%d%d" % (part, b))
                for b in (2, 3):
                    for r in rs:
                        ins = mm(ps[2 + b], "eq", K * b, land, HALF + HALF * r, K, r == 0, r == N - 1)
                    if part == 1:
                        sig(ins, "sum%d" % b)
                for r in rs:
                    for b in range(2):
                        o = T.acc[:, AW * b + HALF * r:AW * b + HALF * r + HALF]
                        i = ps[2 * part + b][:, HALF * (r % 4):HALF * (r % 4) + HALF]
                        wait("V", "un%d%d" % (part, b))
                        if r == 0:
                            sig(V.tensor_copy(o, i), "ad%d" % b)
                            continue
                        wait("V", "haz", "ad%d" % b)
                        if r == N - 1:
                            o = T.ha[:, a + b:a + 256:4]
                        sig(V.tensor_tensor(o, T.acc[:, AW * b + HALF * (r - 1):AW * b + HALF * r], i, A.add),
                            "ad%d" % b if r < N - 1 else "ha")
            for b in (2, 3):
                wait("S", "haz", "sum%d" % b)
                sig(S.activation(T.ha[:, a + b:a + 256:4], ps[2 + b][:, HALF:K], ACT.Copy, scale=1.0 / N), "ha")
            wait("V", "ha")
            sig(quant(nb, K * half, K, T.ha[:]), "qa")
            i = own[half].index(rank)
            rest = [r for r in range(N) if r not in own[0] + own[1]]
            other = [own[1 - half][i]]
            wait("G", "qa")
            for to in ([rest[2 * i:2 * i + 2] + other] if last else [other, rest[2 * i:2 * i + 2]]):
                for codes in (True, False):
                    v = side(nb, HALF + HALF * half, HALF, codes)
                    g.remote_dma_fused([RemoteDMATransfer(dst_ids=[dst(r) for r in to], dma_engine_mask=maskof(engs),
                                                          remote_sem=T.sem["arr" + u], srcs=[v], dsts=[v for r in to])],
                                       local_sem=sem("sent"))
                    count["sent"] += 2 * nh
            wait("P", "ha")

        wait("P", "pc", "psc", "pa" + u, "val")
        for b in range(4):
            mm(ps[b], "eq", K * b, pk, 0, K, True, False)
        wait("V", "sct")
        sig(V.tensor_tensor(T.win2[:], T.win[:, C * t:C * t + C], T.jk[:, 0:C], A.max), "w2")
        wait("V", "w2")
        sig(V.tensor_tensor_scan(T.sr2[:], T.mrow[:], T.win2[:], 0.0, A.add, A.min), "st")
        wait("V", "st")
        sig(V.tensor_scalar(offt[:], T.sr2[:, 15:C:16], off0, STEP, A.add, A.mult), "ot")

        count["arr" + u] = (2 if half is None else 1) * 4 * nh
        if half is not None:
            wait("P", "qa")
        wait("P", "arr" + u)
        for b in range(4):
            sig(mm(ps[b], "eq", K * b, nb, HALF, K, False, True), "dv%d" % b)
        if last:
            wait("P", "wq")
            for o in range(2):
                sig(mm(ps[4 + o], "wq", K * o, nb, HALF, K), "yb%d" % o)
        for b in range(4):
            q = "S" if b % 2 == 0 else "V"
            wait(q, "dv%d" % b)
            if q == "S":
                sig(S.activation(T.hv[:, b:512:4], ps[b][:, 0:K], ACT.Copy, scale=0.5), "hv")
            else:
                sig(V.tensor_scalar(T.hv[:, b:512:4], ps[b][:, 0:K], 0.5, None, A.mult), "hv")
        wait("V", "hv", "ot")
        sig(quant(tv, C, K, T.hv[:]), "qv")
        if last:
            for o in range(2):
                wait("S", "yb%d" % o)
                sig(S.activation(T.ys[:, W * o + C:W * o + W], ps[4 + o][:, 0:K], ACT.Copy), "cb%d" % o)
                wait("Y", "cb%d" % o)
                sig(Y.dma_start(T.y[:, W * o + C:W * o + W], T.ys[:, W * o + C:W * o + W]), "outy", 16)
        wait("V", "qv")
        wait("S", "ot", "qv")
        for a, n, nx in ((0, K, "t%d" % (t + 1)), (K, C - K, "u%d" % (t + 1))):
            sig(pickc(nxt, a, n, tv, W, offt[:, a // 16:(a + n) // 16]), nx)
            sig(picks(nxt, a, n, tv, W, offt[:, a // 16:(a + n) // 16]), nx)

    wait("P", "t2")
    for o in range(2):
        sig(mm(ps[o], "wq", K * o, "tv2", 0, K), "yt%d" % o)
    wait("P", "u2")
    for o in range(2):
        sig(mm(ps[2 + o], "wq", K * o, "tv2", HALF, K), "yu%d" % o)
    wait("Y", "t2", "u2")
    sig(Y.dma_start(T.oc[:], T.tv2[:].bitcast(dt.uint8)), "outy", 16)
    for k in range(2):
        sig(Y.dma_start(T.osc[4 * k:4 * k + 4, :], T.tv2s[32 * k:32 * k + 4, :]), "outy", 16)
    wait("V", "yt0")
    sig(V.tensor_copy(T.ys[:, 0:K], ps[0][:, 0:K]), "cy0")
    wait("V", "yu0")
    sig(V.tensor_copy(T.ys[:, K:C], ps[2][:, HALF:K]), "cy0")
    wait("S", "yt1")
    sig(S.activation(T.ys[:, W:W + K], ps[1][:, 0:K], ACT.Copy), "cy1")
    wait("S", "yu1")
    sig(S.activation(T.ys[:, W + K:W + C], ps[3][:, HALF:K], ACT.Copy), "cy1")
    wait("Y", "cy0")
    sig(Y.dma_start(T.y[:, 0:C], T.ys[:, 0:C]), "outy", 16)
    wait("S", "cy1")
    sig(S.dma_start(T.y[:, W:W + C], T.ys[:, W:W + C]), "outs", 16)
    wait("S", "t2", "u2")
    for k in range(2, 4):
        sig(S.dma_start(T.osc[4 * k:4 * k + 4, :], T.tv2s[32 * k:32 * k + 4, :]), "outs", 16)
    wait("Y", "outy")
    wait("S", "outs")
    for name in list(count):
        if done.get(name, 0) < count[name]:
            wait("G", name)
